import numpy as np
import ml_dtypes


def mxq(x, axis, fmt="e4m3"):
    dtype, down = {"e4m3": (ml_dtypes.float8_e4m3fn, 7), "e5m2": (ml_dtypes.float8_e5m2, 14)}[fmt]
    v = np.moveaxis(np.asarray(x, np.float32).astype(ml_dtypes.bfloat16).astype(np.float64), axis, -1)
    blocks = v.reshape(v.shape[:-1] + (-1, 32))
    amax = np.abs(blocks).max(-1, keepdims=True)
    byte = np.maximum(np.where(amax > 0, np.frexp(amax)[1] - 1 + 127, 0) - down, 1)
    scale = np.exp2(byte - 127.0)
    codes = (blocks / scale).astype(np.float32).astype(dtype).astype(np.float64)
    return np.moveaxis((codes * scale).reshape(v.shape), -1, axis)


WIDE = False


def mx_kscale(k):
    if not WIDE:
        return np.ones(k)
    levels = np.array([10, -10, 5, -5, 0])
    if k % 512:
        return np.exp2(np.random.permutation(np.resize(levels, k // 32))).repeat(32)
    a = np.empty((k // 512, 16))
    for p in range(k // 512):
        a[p, :8] = np.random.permutation(np.resize(levels, 8))
        for g in range(8):
            far = levels[np.abs(levels - a[p, g]) >= 10]
            a[p, g + 8] = far[np.random.randint(len(far))]
    return np.exp2(a.ravel()).repeat(32)


def f64(x):
    return np.asarray(x).astype(np.float64)


def striped(idx):
    return np.tile(np.asarray(idx).reshape(-1, 16).T, (8, 1)).astype(np.uint16)


def unstriped(offs):
    return offs[:16].T.reshape(-1).astype(np.int64)


E2M1 = np.array([0.0, 0.5, 1.0, 1.5, 2.0, 3.0, 4.0, 6.0, -0.0, -0.5, -1.0, -1.5, -2.0, -3.0, -4.0, -6.0])


def pack_weight(w, fmt):
    k, n = w.shape
    w = f64(np.asarray(w, np.float32).astype(ml_dtypes.bfloat16)).reshape(k // 32, 32, n)
    amax = np.abs(w).max(1)
    if fmt == "e4m3":
        byte = np.frexp(amax)[1] - 1 + 127 - 7
    else:
        mant, ex = np.frexp(amax / 6.0)
        byte = np.where(mant > 0.5, ex, ex - 1) + 127
    byte = np.clip(np.where(amax > 0, byte, 1), 1, 254)
    scaled = (w * np.exp2(127.0 - byte)[:, None, :]).reshape(k, n).astype(np.float32)
    by_word = np.ascontiguousarray(scaled.reshape(k // 512, 128, 4, n).transpose(0, 1, 3, 2))
    if fmt == "e4m3":
        words = by_word.astype(ml_dtypes.float8_e4m3fn).view(np.uint8)
    else:
        c = by_word.astype(ml_dtypes.float4_e2m1fn).view(np.uint8) & 0xF
        words = (c[..., 0::2] | (c[..., 1::2] << 4)).reshape(k // 512, 128, 2 * n)
    return np.ascontiguousarray(words), np.ascontiguousarray(byte.astype(np.uint8).reshape(k // 512, 16, n))


def unpack_weight(words, scales, fmt):
    g, _, n = scales.shape
    words = np.ascontiguousarray(words).reshape(g, 128, n, -1)
    if fmt == "e4m3":
        vals = words.view(ml_dtypes.float8_e4m3fn).astype(np.float64)
    else:
        nib = np.empty((g, 128, n, 4), np.uint8)
        nib[..., 0::2] = words & 0xF
        nib[..., 1::2] = words >> 4
        vals = E2M1[nib]
    vals = vals * np.repeat(np.exp2(scales.astype(np.float64) - 127.0), 8, axis=1)[..., None]
    return vals.transpose(0, 1, 3, 2).reshape(g * 512, n)


B, N, T, D, NQ = 2, 512, 2048, 512, 128


def setup_inputs():
    n = np.random.standard_normal
    seg = T // B
    idx = np.concatenate([b * seg + np.random.permutation(seg)[:N] for b in range(B)])
    s = mx_kscale(D)[:, None]
    kp = pack_weight(n((D, T)) / s, "e4m3")
    return {
        "qT": (n((B, D, NQ)) * s * (1.00 / np.sqrt(D))).astype(np.float32),
        "k_words": kp[0],
        "k_scales": kp[1],
        "gn": (-np.log(-np.log(np.random.uniform(0.02, 0.98, (B, NQ, N))))).astype(np.float32),
        "offs": striped(idx),
    }


def reference(qT, k_words, k_scales, gn, offs):
    idx = unstriped(offs)
    pick = lambda x, which: x[:, which].reshape(x.shape[0], B, -1).transpose(1, 0, 2)
    k = unpack_weight(k_words, k_scales, "e4m3")
    kg = pick(k, idx)
    qq = mxq(f64(qT), 1, "e4m3")
    a = qq.transpose(0, 2, 1) @ kg
    g = 2.0 * (a + f64(gn))
    m = np.max(g, axis=-1, keepdims=True)
    e = np.exp(g - m)
    y = e / np.sum(e, axis=-1, keepdims=True)
    return y

@@ -1,0 +1,111 @@
+from contextlib import ExitStack
+
+import concourse.mybir as mybir
+
+B, N, T, D, NQ = 2, 512, 2048, 512, 128
+FLOPS = 2 * B * NQ * N * D
+
+F32 = mybir.dt.float32
+BF16 = mybir.dt.bfloat16
+I32 = mybir.dt.int32
+U32 = mybir.dt.uint32
+U16 = mybir.dt.uint16
+U8 = mybir.dt.uint8
+FP8X4 = mybir.dt.float8_e4m3fn_x4
+ALU = mybir.AluOpType
+ACT = mybir.ActivationFunctionType
+
+P = 128
+PACK = 4
+SEG = T // B
+LIST_COLS = N // 16
+
+
+def tile_attend_gumbel_seg_kernel(tc, qT, k_words, k_scales, gn, offs, out):
+    nc = tc.nc
+    with ExitStack() as ctx:
+        keep = ctx.enter_context(tc.tile_pool(name="keep", bufs=1))
+        psum = ctx.enter_context(tc.psum_pool(name="psum", bufs=1))
+
+        offsets = keep.tile([P, B * LIST_COLS], U16, name="offsets")
+        pool_words = keep.tile([P, T], U32, name="pool_words", align_bytes=64)
+        pool_scales = keep.tile([P, T], U8, name="pool_scales", align_bytes=64)
+        q_raw = [keep.tile([P, PACK, NQ], F32, name=f"q_raw{b}") for b in range(B)]
+        noise = [keep.tile([P, N], F32, name=f"noise{b}") for b in range(B)]
+        warm_in = keep.tile([P, 1], F32, name="warm_in")
+        warm_out = keep.tile([P, 1], F32, name="warm_out")
+
+        nc.vector.memset(pool_scales[:].bitcast(I32), 0)
+        nc.sync.dma_start(offsets[:], offs)
+        scale_rows = k_scales[0].bitcast(I32)
+        for r in range(4):
+            nc.scalar.dma_start(pool_scales[r:P:32, :].bitcast(I32), scale_rows[r:16:4, :])
+        nc.gpsimd.memset(warm_in[:], 0.0)
+        nc.scalar.activation(warm_out[:], warm_in[:], ACT.Exp)
+
+        word_rows = k_words[0].rearrange("p n t -> p (n t)").bitcast(I32)
+        nc.sync.dma_start(pool_words[:, 0:SEG].bitcast(I32), word_rows[:, 0:SEG])
+        for b in range(B):
+            nc.sync.dma_start(q_raw[b][:], qT[b].rearrange("(p j) w -> p j w", j=PACK))
+        nc.sync.dma_start(pool_words[:, SEG:T].bitcast(I32), word_rows[:, SEG:T])
+        for b in range(B):
+            nc.sync.dma_start(noise[b][:], gn[b])
+
+        q_grouped = keep.tile([P, B, NQ, PACK], BF16, name="q_grouped", align_bytes=64)
+        for b in range(B):
+            nc.scalar.copy(q_grouped[:, b, :, :], q_raw[b][:].rearrange("p j w -> p w j"))
+
+        key_scales = keep.tile([P, B * N], U8, name="key_scales", align_bytes=64)
+        key_words = [keep.tile([P, N], U32, name=f"key_words{b}", align_bytes=64) for b in range(B)]
+        q_words = keep.tile([P, B * NQ], U32, name="q_words", align_bytes=64)
+        q_scales = keep.tile([P, B * NQ], U8, name="q_scales", align_bytes=64)
+        scores = [psum.tile([P, N], F32, name=f"scores{b}") for b in range(B)]
+
+        def gather_words(b):
+            window = pool_words[:, 0 : (b + 1) * SEG]
+            listed = offsets[:, b * LIST_COLS : (b + 1) * LIST_COLS]
+            nc.vector.tensor_copy(key_words[b][:], window.indirect(listed))
+
+        def score(b):
+            nc.tensor.matmul_mx(
+                out=scores[b][:],
+                lhsT=q_words[:, b * NQ : (b + 1) * NQ].bitcast(FP8X4),
+                lhsT_scale=q_scales[:, b * NQ : (b + 1) * NQ],
+                rhs=key_words[b][:].bitcast(FP8X4),
+                rhs_scale=key_scales[:, b * N : (b + 1) * N],
+                start=True,
+                stop=True,
+            )
+
+        nc.vector.tensor_copy(key_scales[:], pool_scales[:].indirect(offsets[:]))
+        gather_words(0)
+        nc.vector.quantize_mx(
+            out=q_words[:].bitcast(FP8X4),
+            scales=q_scales[:],
+            in_=q_grouped[:].rearrange("p b w j -> p (b w j)"),
+        )
+        score(0)
+        gather_words(1)
+        score(1)
+
+        summed = [keep.tile([P, N], F32, name=f"summed{b}") for b in range(B)]
+        neg_logits = [keep.tile([P, N], F32, name=f"neg_logits{b}") for b in range(B)]
+        neg_max = [keep.tile([P, 1], F32, name=f"neg_max{b}") for b in range(B)]
+        weights = [keep.tile([P, N], F32, name=f"weights{b}") for b in range(B)]
+        row_sum = [keep.tile([P, 1], F32, name=f"row_sum{b}") for b in range(B)]
+        inv_sum = [keep.tile([P, 1], F32, name=f"inv_sum{b}") for b in range(B)]
+        result = [keep.tile([P, N], F32, name=f"result{b}") for b in range(B)]
+
+        for b in range(B):
+            nc.vector.tensor_tensor(summed[b][:], scores[b][:], noise[b][:], ALU.add)
+        for b in range(B):
+            nc.vector.tensor_scalar(
+                neg_logits[b][:], summed[b][:], -2.0, None, ALU.mult, ALU.min, accum_out=neg_max[b][:]
+            )
+            nc.scalar.activation(
+                weights[b][:], neg_logits[b][:], ACT.Exp, bias=neg_max[b][:], scale=-1.0, accum_out=row_sum[b][:]
+            )
+        for b in range(B):
+            nc.vector.reciprocal(inv_sum[b][:], row_sum[b][:])
+            nc.vector.tensor_scalar(result[b][:], weights[b][:], inv_sum[b][:], None, ALU.mult)
+            nc.sync.dma_start(out[b], result[b][:])

@@ -30,9 +30,8 @@ def tile_attend_gumbel_seg_kernel(tc, qT, k_words, k_scales, gn, offs, out):
         offsets = keep.tile([P, B * LIST_COLS], U16, name="offsets")
         pool_words = keep.tile([P, T], U32, name="pool_words", align_bytes=64)
         pool_scales = keep.tile([P, T], U8, name="pool_scales", align_bytes=64)
-        q_raw = [keep.tile([P, PACK, NQ], F32, name=f"q_raw{b}") for b in range(B)]
-        noise = [keep.tile([P, N], F32, name=f"noise{b}") for b in range(B)]
-        warm_in = keep.tile([P, 1], F32, name="warm_in")
+        q_raw = keep.tile([P, B, PACK * NQ], F32, name="q_raw", tag="q_raw", align_bytes=64)
+        warm_in = keep.tile([P, 1], F32, name="warm_in", tag="noise")
         warm_out = keep.tile([P, 1], F32, name="warm_out")
 
         nc.vector.memset(pool_scales[:].bitcast(I32), 0)
@@ -40,53 +39,56 @@ def tile_attend_gumbel_seg_kernel(tc, qT, k_words, k_scales, gn, offs, out):
         scale_rows = k_scales[0].bitcast(I32)
         for r in range(4):
             nc.scalar.dma_start(pool_scales[r:P:32, :].bitcast(I32), scale_rows[r:16:4, :])
-        nc.gpsimd.memset(warm_in[:], 0.0)
+        nc.vector.memset(warm_in[:], 0.0)
         nc.scalar.activation(warm_out[:], warm_in[:], ACT.Exp)
 
         word_rows = k_words[0].rearrange("p n t -> p (n t)").bitcast(I32)
         nc.sync.dma_start(pool_words[:, 0:SEG].bitcast(I32), word_rows[:, 0:SEG])
-        for b in range(B):
-            nc.sync.dma_start(q_raw[b][:], qT[b].rearrange("(p j) w -> p j w", j=PACK))
         nc.sync.dma_start(pool_words[:, SEG:T].bitcast(I32), word_rows[:, SEG:T])
+        nc.sync.dma_start(q_raw[:], qT.rearrange("b (p j) w -> p b (j w)", j=PACK))
+        noise = keep.tile([P, B, N], F32, name="noise", tag="noise")
         for b in range(B):
-            nc.sync.dma_start(noise[b][:], gn[b])
+            nc.sync.dma_start(noise[:, b, :], gn[b])
 
         q_grouped = keep.tile([P, B, NQ, PACK], BF16, name="q_grouped", align_bytes=64)
         for b in range(B):
-            nc.scalar.copy(q_grouped[:, b, :, :], q_raw[b][:].rearrange("p j w -> p w j"))
+            nc.scalar.copy(q_grouped[:, b, :, :], q_raw[:, b, :].rearrange("p (j w) -> p w j", j=PACK))
 
-        key_scales = keep.tile([P, B * N], U8, name="key_scales", align_bytes=64)
+        key_scales = [
+            keep.tile([P, N], U8, name="key_scales0", align_bytes=64),
+            keep.tile([P, N], U8, name="key_scales1", tag="q_raw", align_bytes=64),
+        ]
         key_words = [keep.tile([P, N], U32, name=f"key_words{b}", align_bytes=64) for b in range(B)]
         q_words = keep.tile([P, B * NQ], U32, name="q_words", align_bytes=64)
         q_scales = keep.tile([P, B * NQ], U8, name="q_scales", align_bytes=64)
-        scores = [psum.tile([P, N], F32, name=f"scores{b}") for b in range(B)]
+        pieces = [(0, 0, N), (1, 0, N // 2), (1, N // 2, N)]
+        scores = [psum.tile([P, hi - lo], F32, name=f"scores{b}_{lo}") for b, lo, hi in pieces]
 
-        def gather_words(b):
-            window = pool_words[:, 0 : (b + 1) * SEG]
-            listed = offsets[:, b * LIST_COLS : (b + 1) * LIST_COLS]
-            nc.vector.tensor_copy(key_words[b][:], window.indirect(listed))
+        def gather(b, lo, hi, pool_tile, gathered):
+            window = pool_tile[:, 0 : (b + 1) * SEG]
+            listed = offsets[:, (b * N + lo) // 16 : (b * N + hi) // 16]
+            nc.vector.tensor_copy(gathered[:, lo:hi], window.indirect(listed))
 
-        def score(b):
-            nc.tensor.matmul_mx(
-                out=scores[b][:],
-                lhsT=q_words[:, b * NQ : (b + 1) * NQ].bitcast(FP8X4),
-                lhsT_scale=q_scales[:, b * NQ : (b + 1) * NQ],
-                rhs=key_words[b][:].bitcast(FP8X4),
-                rhs_scale=key_scales[:, b * N : (b + 1) * N],
-                start=True,
-                stop=True,
-            )
-
-        nc.vector.tensor_copy(key_scales[:], pool_scales[:].indirect(offsets[:]))
-        gather_words(0)
+        for b in range(B):
+            gather(b, 0, N, pool_words, key_words[b])
+        gather(0, 0, N, pool_scales, key_scales[0])
         nc.vector.quantize_mx(
             out=q_words[:].bitcast(FP8X4),
             scales=q_scales[:],
             in_=q_grouped[:].rearrange("p b w j -> p (b w j)"),
         )
-        score(0)
-        gather_words(1)
-        score(1)
+        for piece, (b, lo, hi) in enumerate(pieces):
+            if b == 1:
+                gather(b, lo, hi, pool_scales, key_scales[b])
+            nc.tensor.matmul_mx(
+                out=scores[piece][:],
+                lhsT=q_words[:, b * NQ : (b + 1) * NQ].bitcast(FP8X4),
+                lhsT_scale=q_scales[:, b * NQ : (b + 1) * NQ],
+                rhs=key_words[b][:, lo:hi].bitcast(FP8X4),
+                rhs_scale=key_scales[b][:, lo:hi],
+                start=True,
+                stop=True,
+            )
 
         summed = [keep.tile([P, N], F32, name=f"summed{b}") for b in range(B)]
         neg_logits = [keep.tile([P, N], F32, name=f"neg_logits{b}") for b in range(B)]
@@ -96,8 +98,8 @@ def tile_attend_gumbel_seg_kernel(tc, qT, k_words, k_scales, gn, offs, out):
         inv_sum = [keep.tile([P, 1], F32, name=f"inv_sum{b}") for b in range(B)]
         result = [keep.tile([P, N], F32, name=f"result{b}") for b in range(B)]
 
-        for b in range(B):
-            nc.vector.tensor_tensor(summed[b][:], scores[b][:], noise[b][:], ALU.add)
+        for piece, (b, lo, hi) in enumerate(pieces):
+            nc.vector.tensor_tensor(summed[b][:, lo:hi], scores[piece][:], noise[:, b, lo:hi], ALU.add)
         for b in range(B):
             nc.vector.tensor_scalar(
                 neg_logits[b][:], summed[b][:], -2.0, None, ALU.mult, ALU.min, accum_out=neg_max[b][:]

@@ -30,29 +30,35 @@ def tile_attend_gumbel_seg_kernel(tc, qT, k_words, k_scales, gn, offs, out):
         offsets = keep.tile([P, B * LIST_COLS], U16, name="offsets")
         pool_words = keep.tile([P, T], U32, name="pool_words", align_bytes=64)
         pool_scales = keep.tile([P, T], U8, name="pool_scales", align_bytes=64)
-        q_raw = keep.tile([P, B, PACK * NQ], F32, name="q_raw", tag="q_raw", align_bytes=64)
-        warm_in = keep.tile([P, 1], F32, name="warm_in", tag="noise")
-        warm_out = keep.tile([P, 1], F32, name="warm_out")
+        warm_in = keep.tile([P, 1], F32, name="warm_in", tag="q_raw", align_bytes=64)
+        warm_out = keep.tile([P, 1], F32, name="warm_out", tag="noise")
 
-        nc.vector.memset(pool_scales[:].bitcast(I32), 0)
-        nc.sync.dma_start(offsets[:], offs)
-        scale_rows = k_scales[0].bitcast(I32)
-        for r in range(4):
-            nc.scalar.dma_start(pool_scales[r:P:32, :].bitcast(I32), scale_rows[r:16:4, :])
         nc.vector.memset(warm_in[:], 0.0)
         nc.scalar.activation(warm_out[:], warm_in[:], ACT.Exp)
+        nc.vector.memset(pool_scales[:].bitcast(I32), 0)
+        nc.sync.dma_start(offsets[:], offs)
 
         word_rows = k_words[0].rearrange("p n t -> p (n t)").bitcast(I32)
         nc.sync.dma_start(pool_words[:, 0:SEG].bitcast(I32), word_rows[:, 0:SEG])
         nc.sync.dma_start(pool_words[:, SEG:T].bitcast(I32), word_rows[:, SEG:T])
-        nc.sync.dma_start(q_raw[:], qT.rearrange("b (p j) w -> p b (j w)", j=PACK))
+        scale_rows = k_scales[0].bitcast(I32)
+        for r in range(4):
+            nc.sync.dma_start(pool_scales[r:P:32, :].bitcast(I32), scale_rows[r:16:4, :])
+        q_raw = keep.tile([P, B, PACK, NQ], F32, name="q_raw", tag="q_raw", align_bytes=64)
+        for b in range(B):
+            nc.sync.dma_start(q_raw[:, b, :, :], qT[b].rearrange("(p j) w -> p j w", j=PACK))
         noise = keep.tile([P, B, N], F32, name="noise", tag="noise")
         for b in range(B):
             nc.sync.dma_start(noise[:, b, :], gn[b])
 
         q_grouped = keep.tile([P, B, NQ, PACK], BF16, name="q_grouped", align_bytes=64)
         for b in range(B):
-            nc.scalar.copy(q_grouped[:, b, :, :], q_raw[:, b, :].rearrange("p (j w) -> p w j", j=PACK))
+            nc.scalar.activation(
+                q_grouped[:, b, :, :].rearrange("p (c i) j -> p c j i", i=4),
+                q_raw[:, b, :, :].rearrange("p j (c i) -> p c j i", i=4),
+                ACT.Copy,
+                scale=2.0,
+            )
 
         key_scales = [
             keep.tile([P, N], U8, name="key_scales0", align_bytes=64),
@@ -90,7 +96,6 @@ def tile_attend_gumbel_seg_kernel(tc, qT, k_words, k_scales, gn, offs, out):
                 stop=True,
             )
 
-        summed = [keep.tile([P, N], F32, name=f"summed{b}") for b in range(B)]
         neg_logits = [keep.tile([P, N], F32, name=f"neg_logits{b}") for b in range(B)]
         neg_max = [keep.tile([P, 1], F32, name=f"neg_max{b}") for b in range(B)]
         weights = [keep.tile([P, N], F32, name=f"weights{b}") for b in range(B)]
@@ -99,15 +104,20 @@ def tile_attend_gumbel_seg_kernel(tc, qT, k_words, k_scales, gn, offs, out):
         result = [keep.tile([P, N], F32, name=f"result{b}") for b in range(B)]
 
         for piece, (b, lo, hi) in enumerate(pieces):
-            nc.vector.tensor_tensor(summed[b][:, lo:hi], scores[piece][:], noise[:, b, lo:hi], ALU.add)
-        for b in range(B):
-            nc.vector.tensor_scalar(
-                neg_logits[b][:], summed[b][:], -2.0, None, ALU.mult, ALU.min, accum_out=neg_max[b][:]
+            nc.vector.scalar_tensor_tensor(
+                neg_logits[b][:, lo:hi], noise[:, b, lo:hi], -2.0, scores[piece][:], ALU.mult, ALU.subtract
             )
+        for b in range(B):
+            nc.vector.tensor_reduce(neg_max[b][:], neg_logits[b][:], mybir.AxisListType.X, ALU.min)
             nc.scalar.activation(
                 weights[b][:], neg_logits[b][:], ACT.Exp, bias=neg_max[b][:], scale=-1.0, accum_out=row_sum[b][:]
             )
         for b in range(B):
             nc.vector.reciprocal(inv_sum[b][:], row_sum[b][:])
-            nc.vector.tensor_scalar(result[b][:], weights[b][:], inv_sum[b][:], None, ALU.mult)
-            nc.sync.dma_start(out[b], result[b][:])
+            for piece, (pb, lo, hi) in enumerate(pieces):
+                if pb == b:
+                    nc.vector.tensor_scalar(
+                        result[b][:, lo:hi], weights[b][:, lo:hi], inv_sum[b][:], None, ALU.mult
+                    )
+                    queue = nc.scalar if piece == 2 else nc.sync
+                    queue.dma_start(out[b, :, lo:hi], result[b][:, lo:hi])

@@ -18,7 +18,6 @@ ACT = mybir.ActivationFunctionType
 P = 128
 PACK = 4
 SEG = T // B
-LIST_COLS = N // 16
 
 
 def tile_attend_gumbel_seg_kernel(tc, qT, k_words, k_scales, gn, offs, out):
@@ -27,71 +26,69 @@ def tile_attend_gumbel_seg_kernel(tc, qT, k_words, k_scales, gn, offs, out):
         keep = ctx.enter_context(tc.tile_pool(name="keep", bufs=1))
         psum = ctx.enter_context(tc.psum_pool(name="psum", bufs=1))
 
-        offsets = keep.tile([P, B * LIST_COLS], U16, name="offsets")
-        pool_words = keep.tile([P, T], U32, name="pool_words", align_bytes=64)
+        offsets = keep.tile([P, B * N // 16], U16, name="offsets")
+        first_words = keep.tile([P, SEG], U32, name="first_words", align_bytes=64)
         pool_scales = keep.tile([P, T], U8, name="pool_scales", align_bytes=64)
-        warm_in = keep.tile([P, 1], F32, name="warm_in", tag="q_raw", align_bytes=64)
-        warm_out = keep.tile([P, 1], F32, name="warm_out", tag="noise")
+        warm_in = keep.tile([P, 1], F32, name="warm_in", tag="floats", align_bytes=64)
+        warm_out = keep.tile([P, 1], F32, name="warm_out", tag="second_words", align_bytes=64)
 
         nc.vector.memset(warm_in[:], 0.0)
         nc.scalar.activation(warm_out[:], warm_in[:], ACT.Exp)
         nc.vector.memset(pool_scales[:].bitcast(I32), 0)
-        nc.sync.dma_start(offsets[:], offs)
 
         word_rows = k_words[0].rearrange("p n t -> p (n t)").bitcast(I32)
-        nc.sync.dma_start(pool_words[:, 0:SEG].bitcast(I32), word_rows[:, 0:SEG])
-        nc.sync.dma_start(pool_words[:, SEG:T].bitcast(I32), word_rows[:, SEG:T])
         scale_rows = k_scales[0].bitcast(I32)
+        nc.sync.dma_start(offsets[:], offs)
+        nc.sync.dma_start(first_words[:].bitcast(I32), word_rows[:, 0:SEG])
         for r in range(4):
             nc.sync.dma_start(pool_scales[r:P:32, :].bitcast(I32), scale_rows[r:16:4, :])
-        q_raw = keep.tile([P, B, PACK, NQ], F32, name="q_raw", tag="q_raw", align_bytes=64)
+        floats = keep.tile([P, 2, B, N], F32, name="floats", tag="floats", align_bytes=64)
+        q_raw = [floats[:, 0, b, :] for b in range(B)]
+        noise = [floats[:, 1, b, :] for b in range(B)]
         for b in range(B):
-            nc.sync.dma_start(q_raw[:, b, :, :], qT[b].rearrange("(p j) w -> p j w", j=PACK))
-        noise = keep.tile([P, B, N], F32, name="noise", tag="noise")
+            nc.sync.dma_start(q_raw[b], qT[b].rearrange("(p j) w -> p (j w)", j=PACK))
+        second_words = keep.tile([P, T], U32, name="second_words", tag="second_words", align_bytes=64)
+        nc.sync.dma_start(second_words[:, SEG:T].bitcast(I32), word_rows[:, SEG:T])
         for b in range(B):
-            nc.sync.dma_start(noise[:, b, :], gn[b])
+            nc.sync.dma_start(noise[b], gn[b])
 
         q_grouped = keep.tile([P, B, NQ, PACK], BF16, name="q_grouped", align_bytes=64)
         for b in range(B):
             nc.scalar.activation(
                 q_grouped[:, b, :, :].rearrange("p (c i) j -> p c j i", i=4),
-                q_raw[:, b, :, :].rearrange("p j (c i) -> p c j i", i=4),
+                q_raw[b].rearrange("p (j c i) -> p c j i", j=PACK, i=4),
                 ACT.Copy,
                 scale=2.0,
             )
 
-        key_scales = [
-            keep.tile([P, N], U8, name="key_scales0", align_bytes=64),
-            keep.tile([P, N], U8, name="key_scales1", tag="q_raw", align_bytes=64),
-        ]
+        key_scales = keep.tile([P, B * N], U8, name="key_scales", align_bytes=64)
         key_words = [keep.tile([P, N], U32, name=f"key_words{b}", align_bytes=64) for b in range(B)]
         q_words = keep.tile([P, B * NQ], U32, name="q_words", align_bytes=64)
         q_scales = keep.tile([P, B * NQ], U8, name="q_scales", align_bytes=64)
         pieces = [(0, 0, N), (1, 0, N // 2), (1, N // 2, N)]
         scores = [psum.tile([P, hi - lo], F32, name=f"scores{b}_{lo}") for b, lo, hi in pieces]
+        word_windows = [first_words, second_words]
 
-        def gather(b, lo, hi, pool_tile, gathered):
-            window = pool_tile[:, 0 : (b + 1) * SEG]
+        def gather_words(b, lo, hi):
             listed = offsets[:, (b * N + lo) // 16 : (b * N + hi) // 16]
-            nc.vector.tensor_copy(gathered[:, lo:hi], window.indirect(listed))
+            nc.vector.tensor_copy(key_words[b][:, lo:hi], word_windows[b][:].indirect(listed))
 
-        for b in range(B):
-            gather(b, 0, N, pool_words, key_words[b])
-        gather(0, 0, N, pool_scales, key_scales[0])
+        gather_words(*pieces[0])
+        nc.vector.tensor_copy(key_scales[:], pool_scales[:].indirect(offsets[:]))
         nc.vector.quantize_mx(
             out=q_words[:].bitcast(FP8X4),
             scales=q_scales[:],
             in_=q_grouped[:].rearrange("p b w j -> p (b w j)"),
         )
         for piece, (b, lo, hi) in enumerate(pieces):
-            if b == 1:
-                gather(b, lo, hi, pool_scales, key_scales[b])
+            if piece > 0:
+                gather_words(b, lo, hi)
             nc.tensor.matmul_mx(
                 out=scores[piece][:],
                 lhsT=q_words[:, b * NQ : (b + 1) * NQ].bitcast(FP8X4),
                 lhsT_scale=q_scales[:, b * NQ : (b + 1) * NQ],
                 rhs=key_words[b][:, lo:hi].bitcast(FP8X4),
-                rhs_scale=key_scales[b][:, lo:hi],
+                rhs_scale=key_scales[:, b * N + lo : b * N + hi],
                 start=True,
                 stop=True,
             )
@@ -105,7 +102,7 @@ def tile_attend_gumbel_seg_kernel(tc, qT, k_words, k_scales, gn, offs, out):
 
         for piece, (b, lo, hi) in enumerate(pieces):
             nc.vector.scalar_tensor_tensor(
-                neg_logits[b][:, lo:hi], noise[:, b, lo:hi], -2.0, scores[piece][:], ALU.mult, ALU.subtract
+                neg_logits[b][:, lo:hi], noise[b][:, lo:hi], -2.0, scores[piece][:], ALU.mult, ALU.subtract
             )
         for b in range(B):
             nc.vector.tensor_reduce(neg_max[b][:], neg_logits[b][:], mybir.AxisListType.X, ALU.min)

@@ -18,6 +18,13 @@ ACT = mybir.ActivationFunctionType
 P = 128
 PACK = 4
 SEG = T // B
+LIST_ROWS = 16
+QUADRANT = 32
+SCALE_ROWS = 4
+LINE = 4
+INV_TEMPERATURE = 2.0
+
+PIECES = [(0, 0, N), (1, 0, N // 2), (1, N // 2, N)]
 
 
 def tile_attend_gumbel_seg_kernel(tc, qT, k_words, k_scales, gn, offs, out):
@@ -26,61 +33,62 @@ def tile_attend_gumbel_seg_kernel(tc, qT, k_words, k_scales, gn, offs, out):
         keep = ctx.enter_context(tc.tile_pool(name="keep", bufs=1))
         psum = ctx.enter_context(tc.psum_pool(name="psum", bufs=1))
 
-        offsets = keep.tile([P, B * N // 16], U16, name="offsets")
-        first_words = keep.tile([P, SEG], U32, name="first_words", align_bytes=64)
+        offsets = keep.tile([P, B * N // LIST_ROWS], U16, name="offsets")
+        first_words = keep.tile([P, SEG], U32, name="first_words", tag="words_then_noise", align_bytes=64)
         pool_scales = keep.tile([P, T], U8, name="pool_scales", align_bytes=64)
-        warm_in = keep.tile([P, 1], F32, name="warm_in", tag="floats", align_bytes=64)
-        warm_out = keep.tile([P, 1], F32, name="warm_out", tag="second_words", align_bytes=64)
 
-        nc.vector.memset(warm_in[:], 0.0)
-        nc.scalar.activation(warm_out[:], warm_in[:], ACT.Exp)
-        nc.vector.memset(pool_scales[:].bitcast(I32), 0)
+        nc.vector.memset(pool_scales[:, 0:SEG].bitcast(I32), 0)
+        nc.gpsimd.memset(pool_scales[:, SEG:T].bitcast(I32), 0)
 
         word_rows = k_words[0].rearrange("p n t -> p (n t)").bitcast(I32)
         scale_rows = k_scales[0].bitcast(I32)
+        for lo in (0, SEG // 2):
+            nc.sync.dma_start(first_words[:, lo : lo + SEG // 2].bitcast(I32), word_rows[:, lo : lo + SEG // 2])
         nc.sync.dma_start(offsets[:], offs)
-        nc.sync.dma_start(first_words[:].bitcast(I32), word_rows[:, 0:SEG])
-        for r in range(4):
-            nc.sync.dma_start(pool_scales[r:P:32, :].bitcast(I32), scale_rows[r:16:4, :])
-        floats = keep.tile([P, 2, B, N], F32, name="floats", tag="floats", align_bytes=64)
-        q_raw = [floats[:, 0, b, :] for b in range(B)]
-        noise = [floats[:, 1, b, :] for b in range(B)]
+        for r in range(SCALE_ROWS):
+            nc.sync.dma_start(
+                pool_scales[r:P:QUADRANT, :].bitcast(I32), scale_rows[r : D // 32 : SCALE_ROWS, :]
+            )
+        q_raw = keep.tile([P, B, PACK * NQ], F32, name="q_raw", tag="q_raw_then_keys", align_bytes=64)
         for b in range(B):
-            nc.sync.dma_start(q_raw[b], qT[b].rearrange("(p j) w -> p (j w)", j=PACK))
-        second_words = keep.tile([P, T], U32, name="second_words", tag="second_words", align_bytes=64)
+            nc.sync.dma_start(q_raw[:, b, :], qT[b].rearrange("(p j) w -> p (j w)", j=PACK))
+        second_words = keep.tile([P, T], U32, name="second_words", align_bytes=64)
         nc.sync.dma_start(second_words[:, SEG:T].bitcast(I32), word_rows[:, SEG:T])
-        for b in range(B):
-            nc.sync.dma_start(noise[b], gn[b])
 
         q_grouped = keep.tile([P, B, NQ, PACK], BF16, name="q_grouped", align_bytes=64)
         for b in range(B):
             nc.scalar.activation(
-                q_grouped[:, b, :, :].rearrange("p (c i) j -> p c j i", i=4),
-                q_raw[b].rearrange("p (j c i) -> p c j i", j=PACK, i=4),
+                q_grouped[:, b, :, :].rearrange("p (c i) j -> p c j i", i=LINE),
+                q_raw[:, b, :].rearrange("p (j c i) -> p c j i", j=PACK, i=LINE),
                 ACT.Copy,
-                scale=2.0,
+                scale=INV_TEMPERATURE,
             )
 
         key_scales = keep.tile([P, B * N], U8, name="key_scales", align_bytes=64)
-        key_words = [keep.tile([P, N], U32, name=f"key_words{b}", align_bytes=64) for b in range(B)]
+        key_words = [
+            keep.tile([P, N], U32, name="key_words0", align_bytes=64),
+            keep.tile([P, N], U32, name="key_words1", tag="q_raw_then_keys", align_bytes=64),
+        ]
         q_words = keep.tile([P, B * NQ], U32, name="q_words", align_bytes=64)
         q_scales = keep.tile([P, B * NQ], U8, name="q_scales", align_bytes=64)
-        pieces = [(0, 0, N), (1, 0, N // 2), (1, N // 2, N)]
-        scores = [psum.tile([P, hi - lo], F32, name=f"scores{b}_{lo}") for b, lo, hi in pieces]
+        scores = [psum.tile([P, hi - lo], F32, name=f"scores{b}_{lo}") for b, lo, hi in PIECES]
         word_windows = [first_words, second_words]
 
         def gather_words(b, lo, hi):
-            listed = offsets[:, (b * N + lo) // 16 : (b * N + hi) // 16]
+            listed = offsets[:, (b * N + lo) // LIST_ROWS : (b * N + hi) // LIST_ROWS]
             nc.vector.tensor_copy(key_words[b][:, lo:hi], word_windows[b][:].indirect(listed))
 
-        gather_words(*pieces[0])
+        gather_words(*PIECES[0])
+        noise = keep.tile([P, B, N], F32, name="noise", tag="words_then_noise", align_bytes=64)
+        for b in range(B):
+            nc.sync.dma_start(noise[:, b, :], gn[b])
         nc.vector.tensor_copy(key_scales[:], pool_scales[:].indirect(offsets[:]))
         nc.vector.quantize_mx(
             out=q_words[:].bitcast(FP8X4),
             scales=q_scales[:],
             in_=q_grouped[:].rearrange("p b w j -> p (b w j)"),
         )
-        for piece, (b, lo, hi) in enumerate(pieces):
+        for piece, (b, lo, hi) in enumerate(PIECES):
             if piece > 0:
                 gather_words(b, lo, hi)
             nc.tensor.matmul_mx(
@@ -100,9 +108,14 @@ def tile_attend_gumbel_seg_kernel(tc, qT, k_words, k_scales, gn, offs, out):
         inv_sum = [keep.tile([P, 1], F32, name=f"inv_sum{b}") for b in range(B)]
         result = [keep.tile([P, N], F32, name=f"result{b}") for b in range(B)]
 
-        for piece, (b, lo, hi) in enumerate(pieces):
+        for piece, (b, lo, hi) in enumerate(PIECES):
             nc.vector.scalar_tensor_tensor(
-                neg_logits[b][:, lo:hi], noise[b][:, lo:hi], -2.0, scores[piece][:], ALU.mult, ALU.subtract
+                neg_logits[b][:, lo:hi],
+                noise[:, b, lo:hi],
+                -INV_TEMPERATURE,
+                scores[piece][:],
+                ALU.mult,
+                ALU.subtract,
             )
         for b in range(B):
             nc.vector.tensor_reduce(neg_max[b][:], neg_logits[b][:], mybir.AxisListType.X, ALU.min)
@@ -111,10 +124,10 @@ def tile_attend_gumbel_seg_kernel(tc, qT, k_words, k_scales, gn, offs, out):
             )
         for b in range(B):
             nc.vector.reciprocal(inv_sum[b][:], row_sum[b][:])
-            for piece, (pb, lo, hi) in enumerate(pieces):
-                if pb == b:
+            for piece, (piece_b, lo, hi) in enumerate(PIECES):
+                if piece_b == b:
                     nc.vector.tensor_scalar(
                         result[b][:, lo:hi], weights[b][:, lo:hi], inv_sum[b][:], None, ALU.mult
                     )
-                    queue = nc.scalar if piece == 2 else nc.sync
+                    queue = nc.scalar if piece == len(PIECES) - 1 else nc.sync
                     queue.dma_start(out[b, :, lo:hi], result[b][:, lo:hi])

@@ -34,69 +34,83 @@ def tile_attend_gumbel_seg_kernel(tc, qT, k_words, k_scales, gn, offs, out):
         psum = ctx.enter_context(tc.psum_pool(name="psum", bufs=1))
 
         offsets = keep.tile([P, B * N // LIST_ROWS], U16, name="offsets")
-        first_words = keep.tile([P, SEG], U32, name="first_words", tag="words_then_noise", align_bytes=64)
-        pool_scales = keep.tile([P, T], U8, name="pool_scales", align_bytes=64)
+        word_windows = [keep.tile([P, (b + 1) * SEG], U32, name=f"word_window{b}", align_bytes=64) for b in range(B)]
+        scale_windows = [keep.tile([P, (b + 1) * SEG], U8, name=f"scale_window{b}", align_bytes=64) for b in range(B)]
 
-        nc.vector.memset(pool_scales[:, 0:SEG].bitcast(I32), 0)
-        nc.gpsimd.memset(pool_scales[:, SEG:T].bitcast(I32), 0)
+        nc.vector.memset(scale_windows[1][:, SEG:T].bitcast(I32), 0)
 
         word_rows = k_words[0].rearrange("p n t -> p (n t)").bitcast(I32)
         scale_rows = k_scales[0].bitcast(I32)
-        for lo in (0, SEG // 2):
-            nc.sync.dma_start(first_words[:, lo : lo + SEG // 2].bitcast(I32), word_rows[:, lo : lo + SEG // 2])
+        half = SEG // PACK
         nc.sync.dma_start(offsets[:], offs)
+        for quad in range(P // QUADRANT):
+            rows = scale_rows[SCALE_ROWS * quad : SCALE_ROWS * (quad + 1), 0:half]
+            nc.sync.dma_start(
+                scale_windows[0][QUADRANT * quad : QUADRANT * (quad + 1), :].bitcast(I32),
+                rows.partition_broadcast(QUADRANT // SCALE_ROWS),
+            )
+        nc.sync.dma_start(word_windows[0][:].bitcast(I32), word_rows[:, 0:SEG])
+        q_raw = [keep.tile([P, PACK * NQ], F32, name=f"q_raw{b}", tag=f"q_raw{b}", align_bytes=64) for b in range(B)]
+
+        def load_queries(b):
+            nc.sync.dma_start(q_raw[b][:], qT[b].rearrange("(p j) w -> p (j w)", j=PACK))
+
+        load_queries(0)
         for r in range(SCALE_ROWS):
             nc.sync.dma_start(
-                pool_scales[r:P:QUADRANT, :].bitcast(I32), scale_rows[r : D // 32 : SCALE_ROWS, :]
+                scale_windows[1][r:P:QUADRANT, SEG:T].bitcast(I32),
+                scale_rows[r : D // 32 : SCALE_ROWS, half : 2 * half],
             )
-        q_raw = keep.tile([P, B, PACK * NQ], F32, name="q_raw", tag="q_raw_then_keys", align_bytes=64)
-        for b in range(B):
-            nc.sync.dma_start(q_raw[:, b, :], qT[b].rearrange("(p j) w -> p (j w)", j=PACK))
-        second_words = keep.tile([P, T], U32, name="second_words", align_bytes=64)
-        nc.sync.dma_start(second_words[:, SEG:T].bitcast(I32), word_rows[:, SEG:T])
+        load_queries(1)
+        nc.sync.dma_start(word_windows[1][:, SEG:T].bitcast(I32), word_rows[:, SEG:T])
+        noise = [keep.tile([P, N], F32, name=f"noise{b}") for b in range(B)]
+        for b, lo, hi in PIECES:
+            nc.sync.dma_start(noise[b][:, lo:hi], gn[b, :, lo:hi])
 
-        q_grouped = keep.tile([P, B, NQ, PACK], BF16, name="q_grouped", align_bytes=64)
+        q_grouped = [
+            keep.tile([P, NQ, PACK], BF16, name=f"q_grouped{b}", tag=f"q_grouped{b}", align_bytes=64) for b in range(B)
+        ]
         for b in range(B):
             nc.scalar.activation(
-                q_grouped[:, b, :, :].rearrange("p (c i) j -> p c j i", i=LINE),
-                q_raw[:, b, :].rearrange("p (j c i) -> p c j i", j=PACK, i=LINE),
+                q_grouped[b][:].rearrange("p (c i) j -> p c j i", i=LINE),
+                q_raw[b][:].rearrange("p (j c i) -> p c j i", j=PACK, i=LINE),
                 ACT.Copy,
                 scale=INV_TEMPERATURE,
             )
 
-        key_scales = keep.tile([P, B * N], U8, name="key_scales", align_bytes=64)
-        key_words = [
-            keep.tile([P, N], U32, name="key_words0", align_bytes=64),
-            keep.tile([P, N], U32, name="key_words1", tag="q_raw_then_keys", align_bytes=64),
-        ]
-        q_words = keep.tile([P, B * NQ], U32, name="q_words", align_bytes=64)
-        q_scales = keep.tile([P, B * NQ], U8, name="q_scales", align_bytes=64)
+        def listed(b, lo, hi):
+            return offsets[:, (b * N + lo) // LIST_ROWS : (b * N + hi) // LIST_ROWS]
+
+        key_words = [keep.tile([P, N], U32, name=f"key_words{b}", align_bytes=64) for b in range(B)]
+        key_scales = [keep.tile([P, N], U8, name=f"key_scales{b}", align_bytes=64) for b in range(B)]
+        q_words = [keep.tile([P, NQ], U32, name=f"q_words{b}", align_bytes=64) for b in range(B)]
+        q_scales = [keep.tile([P, NQ], U8, name=f"q_scales{b}", align_bytes=64) for b in range(B)]
         scores = [psum.tile([P, hi - lo], F32, name=f"scores{b}_{lo}") for b, lo, hi in PIECES]
-        word_windows = [first_words, second_words]
 
         def gather_words(b, lo, hi):
-            listed = offsets[:, (b * N + lo) // LIST_ROWS : (b * N + hi) // LIST_ROWS]
-            nc.vector.tensor_copy(key_words[b][:, lo:hi], word_windows[b][:].indirect(listed))
+            nc.vector.tensor_copy(key_words[b][:, lo:hi], word_windows[b][:].indirect(listed(b, lo, hi)))
 
+        def gather_scales(b):
+            nc.vector.tensor_copy(key_scales[b][:], scale_windows[b][:].indirect(listed(b, 0, N)))
+
+        gather_scales(0)
         gather_words(*PIECES[0])
-        noise = keep.tile([P, B, N], F32, name="noise", tag="words_then_noise", align_bytes=64)
+        gather_scales(1)
         for b in range(B):
-            nc.sync.dma_start(noise[:, b, :], gn[b])
-        nc.vector.tensor_copy(key_scales[:], pool_scales[:].indirect(offsets[:]))
-        nc.vector.quantize_mx(
-            out=q_words[:].bitcast(FP8X4),
-            scales=q_scales[:],
-            in_=q_grouped[:].rearrange("p b w j -> p (b w j)"),
-        )
+            nc.vector.quantize_mx(
+                out=q_words[b][:].bitcast(FP8X4),
+                scales=q_scales[b][:],
+                in_=q_grouped[b][:].rearrange("p w j -> p (w j)"),
+            )
         for piece, (b, lo, hi) in enumerate(PIECES):
             if piece > 0:
                 gather_words(b, lo, hi)
             nc.tensor.matmul_mx(
                 out=scores[piece][:],
-                lhsT=q_words[:, b * NQ : (b + 1) * NQ].bitcast(FP8X4),
-                lhsT_scale=q_scales[:, b * NQ : (b + 1) * NQ],
+                lhsT=q_words[b][:].bitcast(FP8X4),
+                lhsT_scale=q_scales[b][:],
                 rhs=key_words[b][:, lo:hi].bitcast(FP8X4),
-                rhs_scale=key_scales[:, b * N + lo : b * N + hi],
+                rhs_scale=key_scales[b][:, lo:hi],
                 start=True,
                 stop=True,
             )
@@ -111,7 +125,7 @@ def tile_attend_gumbel_seg_kernel(tc, qT, k_words, k_scales, gn, offs, out):
         for piece, (b, lo, hi) in enumerate(PIECES):
             nc.vector.scalar_tensor_tensor(
                 neg_logits[b][:, lo:hi],
-                noise[:, b, lo:hi],
+                noise[b][:, lo:hi],
                 -INV_TEMPERATURE,
                 scores[piece][:],
                 ALU.mult,

@@ -24,7 +24,10 @@ SCALE_ROWS = 4
 LINE = 4
 INV_TEMPERATURE = 2.0
 
-PIECES = [(0, 0, N), (1, 0, N // 2), (1, N // 2, N)]
+HALF = N // 2
+
+PIECES = [(0, 0, HALF), (0, HALF, N), (1, 0, HALF), (1, HALF, 3 * N // 4), (1, 3 * N // 4, N)]
+STORES = [(0, 0, N), (1, 0, HALF), (1, HALF, N)]
 
 
 def tile_attend_gumbel_seg_kernel(tc, qT, k_words, k_scales, gn, offs, out):
@@ -63,9 +66,11 @@ def tile_attend_gumbel_seg_kernel(tc, qT, k_words, k_scales, gn, offs, out):
             )
         load_queries(1)
         nc.sync.dma_start(word_windows[1][:, SEG:T].bitcast(I32), word_rows[:, SEG:T])
-        noise = [keep.tile([P, N], F32, name=f"noise{b}") for b in range(B)]
-        for b, lo, hi in PIECES:
-            nc.sync.dma_start(noise[b][:, lo:hi], gn[b, :, lo:hi])
+        noise_loads = [(0, 0, HALF), (0, HALF, N), (1, 0, N)]
+        noise_tiles = [keep.tile([P, hi - lo], F32, name=f"noise{b}_{lo}") for b, lo, hi in noise_loads]
+        for tile, (b, lo, hi) in zip(noise_tiles, noise_loads):
+            nc.sync.dma_start(tile[:], gn[b, :, lo:hi])
+        noise = [noise_tiles[0][:], noise_tiles[1][:]] + [noise_tiles[2][:, lo:hi] for b, lo, hi in PIECES[2:]]
 
         q_grouped = [
             keep.tile([P, NQ, PACK], BF16, name=f"q_grouped{b}", tag=f"q_grouped{b}", align_bytes=64) for b in range(B)
@@ -94,7 +99,7 @@ def tile_attend_gumbel_seg_kernel(tc, qT, k_words, k_scales, gn, offs, out):
             nc.vector.tensor_copy(key_scales[b][:], scale_windows[b][:].indirect(listed(b, 0, N)))
 
         gather_scales(0)
-        gather_words(*PIECES[0])
+        gather_words(0, 0, N)
         gather_scales(1)
         for b in range(B):
             nc.vector.quantize_mx(
@@ -103,7 +108,7 @@ def tile_attend_gumbel_seg_kernel(tc, qT, k_words, k_scales, gn, offs, out):
                 in_=q_grouped[b][:].rearrange("p w j -> p (w j)"),
             )
         for piece, (b, lo, hi) in enumerate(PIECES):
-            if piece > 0:
+            if b > 0:
                 gather_words(b, lo, hi)
             nc.tensor.matmul_mx(
                 out=scores[piece][:],
@@ -116,21 +121,28 @@ def tile_attend_gumbel_seg_kernel(tc, qT, k_words, k_scales, gn, offs, out):
             )
 
         neg_logits = [keep.tile([P, N], F32, name=f"neg_logits{b}") for b in range(B)]
-        neg_max = [keep.tile([P, 1], F32, name=f"neg_max{b}") for b in range(B)]
         weights = [keep.tile([P, N], F32, name=f"weights{b}") for b in range(B)]
         row_sum = [keep.tile([P, 1], F32, name=f"row_sum{b}") for b in range(B)]
         inv_sum = [keep.tile([P, 1], F32, name=f"inv_sum{b}") for b in range(B)]
         result = [keep.tile([P, N], F32, name=f"result{b}") for b in range(B)]
 
-        for piece, (b, lo, hi) in enumerate(PIECES):
+        noise_factor = keep.tile([P, 1], F32, name="noise_factor", tag="noise_factor")
+        nc.vector.memset(noise_factor[:], -INV_TEMPERATURE)
+        first_scores = keep.tile([P, HALF], F32, name="first_scores")
+        first_noise = keep.tile([P, HALF], F32, name="first_noise", tag="first_noise")
+        nc.scalar.copy(first_scores[:], scores[0][:])
+        nc.scalar.activation(first_noise[:], noise[0], ACT.Copy, scale=-INV_TEMPERATURE)
+        nc.gpsimd.tensor_tensor(neg_logits[0][:, 0:HALF], first_noise[:], first_scores[:], ALU.subtract)
+        for piece, (b, lo, hi) in list(enumerate(PIECES))[1:]:
             nc.vector.scalar_tensor_tensor(
                 neg_logits[b][:, lo:hi],
-                noise[b][:, lo:hi],
-                -INV_TEMPERATURE,
+                noise[piece],
+                noise_factor[:] if piece == len(PIECES) - 2 else -INV_TEMPERATURE,
                 scores[piece][:],
                 ALU.mult,
                 ALU.subtract,
             )
+        neg_max = [keep.tile([P, 1], F32, name="neg_max0", tag="noise_factor"), keep.tile([P, 1], F32, name="neg_max1", tag="first_noise")]
         for b in range(B):
             nc.vector.tensor_reduce(neg_max[b][:], neg_logits[b][:], mybir.AxisListType.X, ALU.min)
             nc.scalar.activation(
@@ -138,10 +150,9 @@ def tile_attend_gumbel_seg_kernel(tc, qT, k_words, k_scales, gn, offs, out):
             )
         for b in range(B):
             nc.vector.reciprocal(inv_sum[b][:], row_sum[b][:])
-            for piece, (piece_b, lo, hi) in enumerate(PIECES):
+            for piece_b, lo, hi in STORES:
                 if piece_b == b:
                     nc.vector.tensor_scalar(
                         result[b][:, lo:hi], weights[b][:, lo:hi], inv_sum[b][:], None, ALU.mult
                     )
-                    queue = nc.scalar if piece == len(PIECES) - 1 else nc.sync
-                    queue.dma_start(out[b, :, lo:hi], result[b][:, lo:hi])
+                    nc.sync.dma_start(out[b, :, lo:hi], result[b][:, lo:hi])

@@ -66,11 +66,13 @@ def tile_attend_gumbel_seg_kernel(tc, qT, k_words, k_scales, gn, offs, out):
             )
         load_queries(1)
         nc.sync.dma_start(word_windows[1][:, SEG:T].bitcast(I32), word_rows[:, SEG:T])
-        noise_loads = [(0, 0, HALF), (0, HALF, N), (1, 0, N)]
+        noise_loads = [(0, HALF, N), (0, 0, HALF), (1, 0, HALF), (1, HALF, N)]
         noise_tiles = [keep.tile([P, hi - lo], F32, name=f"noise{b}_{lo}") for b, lo, hi in noise_loads]
         for tile, (b, lo, hi) in zip(noise_tiles, noise_loads):
             nc.sync.dma_start(tile[:], gn[b, :, lo:hi])
-        noise = [noise_tiles[0][:], noise_tiles[1][:]] + [noise_tiles[2][:, lo:hi] for b, lo, hi in PIECES[2:]]
+        noise = [noise_tiles[1][:], noise_tiles[0][:], noise_tiles[2][:]] + [
+            noise_tiles[3][:, lo - HALF : hi - HALF] for b, lo, hi in PIECES[3:]
+        ]
 
         q_grouped = [
             keep.tile([P, NQ, PACK], BF16, name=f"q_grouped{b}", tag=f"q_grouped{b}", align_bytes=64) for b in range(B)
@@ -87,7 +89,11 @@ def tile_attend_gumbel_seg_kernel(tc, qT, k_words, k_scales, gn, offs, out):
             return offsets[:, (b * N + lo) // LIST_ROWS : (b * N + hi) // LIST_ROWS]
 
         key_words = [keep.tile([P, N], U32, name=f"key_words{b}", align_bytes=64) for b in range(B)]
-        key_scales = [keep.tile([P, N], U8, name=f"key_scales{b}", align_bytes=64) for b in range(B)]
+        scale_runs = [(0, 0, N, "key_scales0"), (1, 0, HALF, "key_scales1"), (1, HALF, N, "q_raw0")]
+        key_scales = [
+            keep.tile([P, hi - lo], U8, name=f"key_scales{b}_{lo}", tag=tag, align_bytes=64)
+            for b, lo, hi, tag in scale_runs
+        ]
         q_words = [keep.tile([P, NQ], U32, name=f"q_words{b}", align_bytes=64) for b in range(B)]
         q_scales = [keep.tile([P, NQ], U8, name=f"q_scales{b}", align_bytes=64) for b in range(B)]
         scores = [psum.tile([P, hi - lo], F32, name=f"scores{b}_{lo}") for b, lo, hi in PIECES]
@@ -95,8 +101,13 @@ def tile_attend_gumbel_seg_kernel(tc, qT, k_words, k_scales, gn, offs, out):
         def gather_words(b, lo, hi):
             nc.vector.tensor_copy(key_words[b][:, lo:hi], word_windows[b][:].indirect(listed(b, lo, hi)))
 
-        def gather_scales(b):
-            nc.vector.tensor_copy(key_scales[b][:], scale_windows[b][:].indirect(listed(b, 0, N)))
+        def gather_scales(run):
+            b, lo, hi, tag = scale_runs[run]
+            nc.vector.tensor_copy(key_scales[run][:], scale_windows[b][:].indirect(listed(b, lo, hi)))
+
+        def scales_of(b, lo, hi):
+            run = [i for i, (rb, rlo, rhi, tag) in enumerate(scale_runs) if rb == b and rlo <= lo < rhi][0]
+            return key_scales[run][:, lo - scale_runs[run][1] : hi - scale_runs[run][1]]
 
         gather_scales(0)
         gather_words(0, 0, N)
@@ -107,6 +118,8 @@ def tile_attend_gumbel_seg_kernel(tc, qT, k_words, k_scales, gn, offs, out):
                 scales=q_scales[b][:],
                 in_=q_grouped[b][:].rearrange("p w j -> p (w j)"),
             )
+            if b == 0:
+                gather_scales(2)
         for piece, (b, lo, hi) in enumerate(PIECES):
             if b > 0:
                 gather_words(b, lo, hi)
@@ -115,7 +128,7 @@ def tile_attend_gumbel_seg_kernel(tc, qT, k_words, k_scales, gn, offs, out):
                 lhsT=q_words[b][:].bitcast(FP8X4),
                 lhsT_scale=q_scales[b][:],
                 rhs=key_words[b][:, lo:hi].bitcast(FP8X4),
-                rhs_scale=key_scales[b][:, lo:hi],
+                rhs_scale=scales_of(b, lo, hi),
                 start=True,
                 stop=True,
             )

@@ -27,7 +27,7 @@ INV_TEMPERATURE = 2.0
 HALF = N // 2
 
 PIECES = [(0, 0, HALF), (0, HALF, N), (1, 0, HALF), (1, HALF, 3 * N // 4), (1, 3 * N // 4, N)]
-STORES = [(0, 0, N), (1, 0, HALF), (1, HALF, N)]
+STORES = [(b, lo, lo + HALF) for b in range(B) for lo in (0, HALF)]
 
 
 def tile_attend_gumbel_seg_kernel(tc, qT, k_words, k_scales, gn, offs, out):

@@ -45,13 +45,13 @@ def tile_attend_gumbel_seg_kernel(tc, qT, k_words, k_scales, gn, offs, out):
         word_rows = k_words[0].rearrange("p n t -> p (n t)").bitcast(I32)
         scale_rows = k_scales[0].bitcast(I32)
         half = SEG // PACK
-        nc.sync.dma_start(offsets[:], offs)
         for quad in range(P // QUADRANT):
             rows = scale_rows[SCALE_ROWS * quad : SCALE_ROWS * (quad + 1), 0:half]
             nc.sync.dma_start(
                 scale_windows[0][QUADRANT * quad : QUADRANT * (quad + 1), :].bitcast(I32),
                 rows.partition_broadcast(QUADRANT // SCALE_ROWS),
             )
+        nc.sync.dma_start(offsets[:], offs)
         nc.sync.dma_start(word_windows[0][:].bitcast(I32), word_rows[:, 0:SEG])
         q_raw = [keep.tile([P, PACK * NQ], F32, name=f"q_raw{b}", tag=f"q_raw{b}", align_bytes=64) for b in range(B)]
 

@@ -27,7 +27,7 @@ INV_TEMPERATURE = 2.0
 HALF = N // 2
 
 PIECES = [(0, 0, HALF), (0, HALF, N), (1, 0, HALF), (1, HALF, 3 * N // 4), (1, 3 * N // 4, N)]
-STORES = [(b, lo, lo + HALF) for b in range(B) for lo in (0, HALF)]
+STORES = [(b, lo, hi) for b in range(B) for lo, hi in ((0, N // 4), (N // 4, N))]
 
 
 def tile_attend_gumbel_seg_kernel(tc, qT, k_words, k_scales, gn, offs, out):
@@ -69,7 +69,9 @@ def tile_attend_gumbel_seg_kernel(tc, qT, k_words, k_scales, gn, offs, out):
         noise_loads = [(0, HALF, N), (0, 0, HALF), (1, 0, HALF), (1, HALF, N)]
         noise_tiles = [keep.tile([P, hi - lo], F32, name=f"noise{b}_{lo}") for b, lo, hi in noise_loads]
         for tile, (b, lo, hi) in zip(noise_tiles, noise_loads):
-            nc.sync.dma_start(tile[:], gn[b, :, lo:hi])
+            step = (hi - lo) // 2 if b == 0 else hi - lo
+            for first in range(0, hi - lo, step):
+                nc.sync.dma_start(tile[:, first : first + step], gn[b, :, lo + first : lo + first + step])
         noise = [noise_tiles[1][:], noise_tiles[0][:], noise_tiles[2][:]] + [
             noise_tiles[3][:, lo - HALF : hi - HALF] for b, lo, hi in PIECES[3:]
         ]

@@ -26,7 +26,7 @@ INV_TEMPERATURE = 2.0
 
 HALF = N // 2
 
-PIECES = [(0, 0, HALF), (0, HALF, N), (1, 0, HALF), (1, HALF, 3 * N // 4), (1, 3 * N // 4, N)]
+PIECES = [(0, HALF, N), (0, 0, HALF), (1, 0, HALF), (1, HALF, 3 * N // 4), (1, 3 * N // 4, N)]
 STORES = [(b, lo, hi) for b in range(B) for lo, hi in ((0, N // 4), (N // 4, N))]
 
 
@@ -66,15 +66,12 @@ def tile_attend_gumbel_seg_kernel(tc, qT, k_words, k_scales, gn, offs, out):
             )
         load_queries(1)
         nc.sync.dma_start(word_windows[1][:, SEG:T].bitcast(I32), word_rows[:, SEG:T])
-        noise_loads = [(0, HALF, N), (0, 0, HALF), (1, 0, HALF), (1, HALF, N)]
-        noise_tiles = [keep.tile([P, hi - lo], F32, name=f"noise{b}_{lo}") for b, lo, hi in noise_loads]
-        for tile, (b, lo, hi) in zip(noise_tiles, noise_loads):
-            step = (hi - lo) // 2 if b == 0 else hi - lo
-            for first in range(0, hi - lo, step):
-                nc.sync.dma_start(tile[:, first : first + step], gn[b, :, lo + first : lo + first + step])
-        noise = [noise_tiles[1][:], noise_tiles[0][:], noise_tiles[2][:]] + [
-            noise_tiles[3][:, lo - HALF : hi - HALF] for b, lo, hi in PIECES[3:]
-        ]
+        far_noise = keep.tile([P, HALF], F32, name="far_noise")
+        near_noise = keep.tile([P, B, HALF], F32, name="near_noise")
+        last_noise = keep.tile([P, HALF], F32, name="last_noise")
+        nc.sync.dma_start(far_noise[:], gn[0, :, HALF:N])
+        nc.sync.dma_start(near_noise[:], gn[:, :, 0:HALF].rearrange("b p w -> p b w"))
+        nc.sync.dma_start(last_noise[:], gn[1, :, HALF:N])
 
         q_grouped = [
             keep.tile([P, NQ, PACK], BF16, name=f"q_grouped{b}", tag=f"q_grouped{b}", align_bytes=64) for b in range(B)
@@ -98,7 +95,8 @@ def tile_attend_gumbel_seg_kernel(tc, qT, k_words, k_scales, gn, offs, out):
         ]
         q_words = [keep.tile([P, NQ], U32, name=f"q_words{b}", align_bytes=64) for b in range(B)]
         q_scales = [keep.tile([P, NQ], U8, name=f"q_scales{b}", align_bytes=64) for b in range(B)]
-        scores = [psum.tile([P, hi - lo], F32, name=f"scores{b}_{lo}") for b, lo, hi in PIECES]
+        banks = [psum.tile([P, HALF], F32, name=f"scores{b}_{lo}") for b in range(B) for lo in (0, HALF)]
+        scores = [banks[2 * b + lo // HALF][:, lo % HALF : lo % HALF + hi - lo] for b, lo, hi in PIECES]
 
         def gather_words(b, lo, hi):
             nc.vector.tensor_copy(key_words[b][:, lo:hi], word_windows[b][:].indirect(listed(b, lo, hi)))
@@ -126,7 +124,7 @@ def tile_attend_gumbel_seg_kernel(tc, qT, k_words, k_scales, gn, offs, out):
             if b > 0:
                 gather_words(b, lo, hi)
             nc.tensor.matmul_mx(
-                out=scores[piece][:],
+                out=scores[piece],
                 lhsT=q_words[b][:].bitcast(FP8X4),
                 lhsT_scale=q_scales[b][:],
                 rhs=key_words[b][:, lo:hi].bitcast(FP8X4),
@@ -135,33 +133,39 @@ def tile_attend_gumbel_seg_kernel(tc, qT, k_words, k_scales, gn, offs, out):
                 stop=True,
             )
 
-        neg_logits = [keep.tile([P, N], F32, name=f"neg_logits{b}") for b in range(B)]
+        padded = keep.tile([P, N + 1], F32, name="padded")
+        neg_logits = [padded[:, 0:N], keep.tile([P, N], F32, name="neg_logits1")[:]]
+        far_scores = keep.tile([P, HALF], F32, name="far_scores")
+        far_scaled = keep.tile([P, HALF], F32, name="far_scaled")
         weights = [keep.tile([P, N], F32, name=f"weights{b}") for b in range(B)]
         row_sum = [keep.tile([P, 1], F32, name=f"row_sum{b}") for b in range(B)]
         inv_sum = [keep.tile([P, 1], F32, name=f"inv_sum{b}") for b in range(B)]
         result = [keep.tile([P, N], F32, name=f"result{b}") for b in range(B)]
 
-        noise_factor = keep.tile([P, 1], F32, name="noise_factor", tag="noise_factor")
-        nc.vector.memset(noise_factor[:], -INV_TEMPERATURE)
-        first_scores = keep.tile([P, HALF], F32, name="first_scores")
-        first_noise = keep.tile([P, HALF], F32, name="first_noise", tag="first_noise")
-        nc.scalar.copy(first_scores[:], scores[0][:])
-        nc.scalar.activation(first_noise[:], noise[0], ACT.Copy, scale=-INV_TEMPERATURE)
-        nc.gpsimd.tensor_tensor(neg_logits[0][:, 0:HALF], first_noise[:], first_scores[:], ALU.subtract)
-        for piece, (b, lo, hi) in list(enumerate(PIECES))[1:]:
+        nc.scalar.copy(far_scores[:], banks[1][:])
+        nc.scalar.activation(far_scaled[:], far_noise[:], ACT.Copy, scale=-INV_TEMPERATURE)
+        nc.gpsimd.tensor_tensor(neg_logits[0][:, HALF:N], far_scaled[:], far_scores[:], ALU.subtract)
+
+        def add_noise(b, lo, noise):
             nc.vector.scalar_tensor_tensor(
-                neg_logits[b][:, lo:hi],
-                noise[piece],
-                noise_factor[:] if piece == len(PIECES) - 2 else -INV_TEMPERATURE,
-                scores[piece][:],
+                neg_logits[b][:, lo : lo + HALF],
+                noise,
+                -INV_TEMPERATURE,
+                banks[2 * b + lo // HALF][:],
                 ALU.mult,
                 ALU.subtract,
             )
-        neg_max = [keep.tile([P, 1], F32, name="neg_max0", tag="noise_factor"), keep.tile([P, 1], F32, name="neg_max1", tag="first_noise")]
+
         for b in range(B):
-            nc.vector.tensor_reduce(neg_max[b][:], neg_logits[b][:], mybir.AxisListType.X, ALU.min)
+            add_noise(b, 0, near_noise[:, b, :])
+        nc.vector.tensor_reduce(padded[:, N : N + 1], neg_logits[0][:, 0:HALF], mybir.AxisListType.X, ALU.min)
+        add_noise(1, HALF, last_noise[:])
+        neg_max = [keep.tile([P, 1], F32, name=f"neg_max{b}") for b in range(B)]
+        for b in range(B):
+            rest = padded[:, HALF : N + 1] if b == 0 else neg_logits[b]
+            nc.vector.tensor_reduce(neg_max[b][:], rest, mybir.AxisListType.X, ALU.min)
             nc.scalar.activation(
-                weights[b][:], neg_logits[b][:], ACT.Exp, bias=neg_max[b][:], scale=-1.0, accum_out=row_sum[b][:]
+                weights[b][:], neg_logits[b], ACT.Exp, bias=neg_max[b][:], scale=-1.0, accum_out=row_sum[b][:]
             )
         for b in range(B):
             nc.vector.reciprocal(inv_sum[b][:], row_sum[b][:])

@@ -174,4 +174,6 @@ def tile_attend_gumbel_seg_kernel(tc, qT, k_words, k_scales, gn, offs, out):
                     nc.vector.tensor_scalar(
                         result[b][:, lo:hi], weights[b][:, lo:hi], inv_sum[b][:], None, ALU.mult
                     )
-                    nc.sync.dma_start(out[b, :, lo:hi], result[b][:, lo:hi])
+                    parts = 2 if (b, hi) == (B - 1, N) else 1
+                    for first in range(parts):
+                        nc.sync.dma_start(out[b, first:P:parts, lo:hi], result[b][first:P:parts, lo:hi])

@@ -40,18 +40,24 @@ def tile_attend_gumbel_seg_kernel(tc, qT, k_words, k_scales, gn, offs, out):
         word_windows = [keep.tile([P, (b + 1) * SEG], U32, name=f"word_window{b}", align_bytes=64) for b in range(B)]
         scale_windows = [keep.tile([P, (b + 1) * SEG], U8, name=f"scale_window{b}", align_bytes=64) for b in range(B)]
 
+        nc.vector.memset(scale_windows[0][P // 2 : P, :].bitcast(I32), 0)
         nc.vector.memset(scale_windows[1][:, SEG:T].bitcast(I32), 0)
 
         word_rows = k_words[0].rearrange("p n t -> p (n t)").bitcast(I32)
         scale_rows = k_scales[0].bitcast(I32)
         half = SEG // PACK
-        for quad in range(P // QUADRANT):
+        for quad in (0, 1):
             rows = scale_rows[SCALE_ROWS * quad : SCALE_ROWS * (quad + 1), 0:half]
             nc.sync.dma_start(
                 scale_windows[0][QUADRANT * quad : QUADRANT * (quad + 1), :].bitcast(I32),
                 rows.partition_broadcast(QUADRANT // SCALE_ROWS),
             )
         nc.sync.dma_start(offsets[:], offs)
+        for quad in (2, 3):
+            nc.sync.dma_start(
+                scale_windows[0][QUADRANT * quad : QUADRANT * quad + SCALE_ROWS, :].bitcast(I32),
+                scale_rows[SCALE_ROWS * quad : SCALE_ROWS * (quad + 1), 0:half],
+            )
         nc.sync.dma_start(word_windows[0][:].bitcast(I32), word_rows[:, 0:SEG])
         q_raw = [keep.tile([P, PACK * NQ], F32, name=f"q_raw{b}", tag=f"q_raw{b}", align_bytes=64) for b in range(B)]
 

@@ -40,20 +40,20 @@ def tile_attend_gumbel_seg_kernel(tc, qT, k_words, k_scales, gn, offs, out):
         word_windows = [keep.tile([P, (b + 1) * SEG], U32, name=f"word_window{b}", align_bytes=64) for b in range(B)]
         scale_windows = [keep.tile([P, (b + 1) * SEG], U8, name=f"scale_window{b}", align_bytes=64) for b in range(B)]
 
-        nc.vector.memset(scale_windows[0][P // 2 : P, :].bitcast(I32), 0)
+        nc.vector.memset(scale_windows[0][P - QUADRANT : P, :].bitcast(I32), 0)
         nc.vector.memset(scale_windows[1][:, SEG:T].bitcast(I32), 0)
 
         word_rows = k_words[0].rearrange("p n t -> p (n t)").bitcast(I32)
         scale_rows = k_scales[0].bitcast(I32)
         half = SEG // PACK
-        for quad in (0, 1):
+        for quad in (0, 1, 2):
             rows = scale_rows[SCALE_ROWS * quad : SCALE_ROWS * (quad + 1), 0:half]
             nc.sync.dma_start(
                 scale_windows[0][QUADRANT * quad : QUADRANT * (quad + 1), :].bitcast(I32),
                 rows.partition_broadcast(QUADRANT // SCALE_ROWS),
             )
         nc.sync.dma_start(offsets[:], offs)
-        for quad in (2, 3):
+        for quad in (3,):
             nc.sync.dma_start(
                 scale_windows[0][QUADRANT * quad : QUADRANT * quad + SCALE_ROWS, :].bitcast(I32),
                 scale_rows[SCALE_ROWS * quad : SCALE_ROWS * (quad + 1), 0:half],

from contextlib import ExitStack

import concourse.mybir as mybir

B, N, T, D, NQ = 2, 512, 2048, 512, 128
FLOPS = 2 * B * NQ * N * D

F32 = mybir.dt.float32
BF16 = mybir.dt.bfloat16
I32 = mybir.dt.int32
U32 = mybir.dt.uint32
U16 = mybir.dt.uint16
U8 = mybir.dt.uint8
FP8X4 = mybir.dt.float8_e4m3fn_x4
ALU = mybir.AluOpType
ACT = mybir.ActivationFunctionType

P = 128
PACK = 4
SEG = T // B
LIST_ROWS = 16
QUADRANT = 32
SCALE_ROWS = 4
LINE = 4
INV_TEMPERATURE = 2.0

HALF = N // 2

PIECES = [(0, HALF, N), (0, 0, HALF), (1, 0, HALF), (1, HALF, 3 * N // 4), (1, 3 * N // 4, N)]
STORES = [(b, lo, hi) for b in range(B) for lo, hi in ((0, N // 4), (N // 4, N))]


def tile_attend_gumbel_seg_kernel(tc, qT, k_words, k_scales, gn, offs, out):
    nc = tc.nc
    with ExitStack() as ctx:
        keep = ctx.enter_context(tc.tile_pool(name="keep", bufs=1))
        psum = ctx.enter_context(tc.psum_pool(name="psum", bufs=1))

        offsets = keep.tile([P, B * N // LIST_ROWS], U16, name="offsets")
        word_windows = [keep.tile([P, (b + 1) * SEG], U32, name=f"word_window{b}", align_bytes=64) for b in range(B)]
        scale_windows = [keep.tile([P, (b + 1) * SEG], U8, name=f"scale_window{b}", align_bytes=64) for b in range(B)]

        nc.vector.memset(scale_windows[0][P - QUADRANT : P, :].bitcast(I32), 0)
        nc.vector.memset(scale_windows[1][:, SEG:T].bitcast(I32), 0)

        word_rows = k_words[0].rearrange("p n t -> p (n t)").bitcast(I32)
        scale_rows = k_scales[0].bitcast(I32)
        half = SEG // PACK
        for quad in (0, 1, 2):
            rows = scale_rows[SCALE_ROWS * quad : SCALE_ROWS * (quad + 1), 0:half]
            nc.sync.dma_start(
                scale_windows[0][QUADRANT * quad : QUADRANT * (quad + 1), :].bitcast(I32),
                rows.partition_broadcast(QUADRANT // SCALE_ROWS),
            )
        nc.sync.dma_start(offsets[:], offs)
        for quad in (3,):
            nc.sync.dma_start(
                scale_windows[0][QUADRANT * quad : QUADRANT * quad + SCALE_ROWS, :].bitcast(I32),
                scale_rows[SCALE_ROWS * quad : SCALE_ROWS * (quad + 1), 0:half],
            )
        nc.sync.dma_start(word_windows[0][:].bitcast(I32), word_rows[:, 0:SEG])
        q_raw = [keep.tile([P, PACK * NQ], F32, name=f"q_raw{b}", tag=f"q_raw{b}", align_bytes=64) for b in range(B)]

        def load_queries(b):
            nc.sync.dma_start(q_raw[b][:], qT[b].rearrange("(p j) w -> p (j w)", j=PACK))

        load_queries(0)
        for r in range(SCALE_ROWS):
            nc.sync.dma_start(
                scale_windows[1][r:P:QUADRANT, SEG:T].bitcast(I32),
                scale_rows[r : D // 32 : SCALE_ROWS, half : 2 * half],
            )
        load_queries(1)
        nc.sync.dma_start(word_windows[1][:, SEG:T].bitcast(I32), word_rows[:, SEG:T])
        far_noise = keep.tile([P, HALF], F32, name="far_noise")
        near_noise = keep.tile([P, B, HALF], F32, name="near_noise")
        last_noise = keep.tile([P, HALF], F32, name="last_noise")
        nc.sync.dma_start(far_noise[:], gn[0, :, HALF:N])
        nc.sync.dma_start(near_noise[:], gn[:, :, 0:HALF].rearrange("b p w -> p b w"))
        nc.sync.dma_start(last_noise[:], gn[1, :, HALF:N])

        q_grouped = [
            keep.tile([P, NQ, PACK], BF16, name=f"q_grouped{b}", tag=f"q_grouped{b}", align_bytes=64) for b in range(B)
        ]
        for b in range(B):
            nc.scalar.activation(
                q_grouped[b][:].rearrange("p (c i) j -> p c j i", i=LINE),
                q_raw[b][:].rearrange("p (j c i) -> p c j i", j=PACK, i=LINE),
                ACT.Copy,
                scale=INV_TEMPERATURE,
            )

        def listed(b, lo, hi):
            return offsets[:, (b * N + lo) // LIST_ROWS : (b * N + hi) // LIST_ROWS]

        key_words = [keep.tile([P, N], U32, name=f"key_words{b}", align_bytes=64) for b in range(B)]
        scale_runs = [(0, 0, N, "key_scales0"), (1, 0, HALF, "key_scales1"), (1, HALF, N, "q_raw0")]
        key_scales = [
            keep.tile([P, hi - lo], U8, name=f"key_scales{b}_{lo}", tag=tag, align_bytes=64)
            for b, lo, hi, tag in scale_runs
        ]
        q_words = [keep.tile([P, NQ], U32, name=f"q_words{b}", align_bytes=64) for b in range(B)]
        q_scales = [keep.tile([P, NQ], U8, name=f"q_scales{b}", align_bytes=64) for b in range(B)]
        banks = [psum.tile([P, HALF], F32, name=f"scores{b}_{lo}") for b in range(B) for lo in (0, HALF)]
        scores = [banks[2 * b + lo // HALF][:, lo % HALF : lo % HALF + hi - lo] for b, lo, hi in PIECES]

        def gather_words(b, lo, hi):
            nc.vector.tensor_copy(key_words[b][:, lo:hi], word_windows[b][:].indirect(listed(b, lo, hi)))

        def gather_scales(run):
            b, lo, hi, tag = scale_runs[run]
            nc.vector.tensor_copy(key_scales[run][:], scale_windows[b][:].indirect(listed(b, lo, hi)))

        def scales_of(b, lo, hi):
            run = [i for i, (rb, rlo, rhi, tag) in enumerate(scale_runs) if rb == b and rlo <= lo < rhi][0]
            return key_scales[run][:, lo - scale_runs[run][1] : hi - scale_runs[run][1]]

        gather_scales(0)
        gather_words(0, 0, N)
        gather_scales(1)
        for b in range(B):
            nc.vector.quantize_mx(
                out=q_words[b][:].bitcast(FP8X4),
                scales=q_scales[b][:],
                in_=q_grouped[b][:].rearrange("p w j -> p (w j)"),
            )
            if b == 0:
                gather_scales(2)
        for piece, (b, lo, hi) in enumerate(PIECES):
            if b > 0:
                gather_words(b, lo, hi)
            nc.tensor.matmul_mx(
                out=scores[piece],
                lhsT=q_words[b][:].bitcast(FP8X4),
                lhsT_scale=q_scales[b][:],
                rhs=key_words[b][:, lo:hi].bitcast(FP8X4),
                rhs_scale=scales_of(b, lo, hi),
                start=True,
                stop=True,
            )

        padded = keep.tile([P, N + 1], F32, name="padded")
        neg_logits = [padded[:, 0:N], keep.tile([P, N], F32, name="neg_logits1")[:]]
        far_scores = keep.tile([P, HALF], F32, name="far_scores")
        far_scaled = keep.tile([P, HALF], F32, name="far_scaled")
        weights = [keep.tile([P, N], F32, name=f"weights{b}") for b in range(B)]
        row_sum = [keep.tile([P, 1], F32, name=f"row_sum{b}") for b in range(B)]
        inv_sum = [keep.tile([P, 1], F32, name=f"inv_sum{b}") for b in range(B)]
        result = [keep.tile([P, N], F32, name=f"result{b}") for b in range(B)]

        nc.scalar.copy(far_scores[:], banks[1][:])
        nc.scalar.activation(far_scaled[:], far_noise[:], ACT.Copy, scale=-INV_TEMPERATURE)
        nc.gpsimd.tensor_tensor(neg_logits[0][:, HALF:N], far_scaled[:], far_scores[:], ALU.subtract)

        def add_noise(b, lo, noise):
            nc.vector.scalar_tensor_tensor(
                neg_logits[b][:, lo : lo + HALF],
                noise,
                -INV_TEMPERATURE,
                banks[2 * b + lo // HALF][:],
                ALU.mult,
                ALU.subtract,
            )

        for b in range(B):
            add_noise(b, 0, near_noise[:, b, :])
        nc.vector.tensor_reduce(padded[:, N : N + 1], neg_logits[0][:, 0:HALF], mybir.AxisListType.X, ALU.min)
        add_noise(1, HALF, last_noise[:])
        neg_max = [keep.tile([P, 1], F32, name=f"neg_max{b}") for b in range(B)]
        for b in range(B):
            rest = padded[:, HALF : N + 1] if b == 0 else neg_logits[b]
            nc.vector.tensor_reduce(neg_max[b][:], rest, mybir.AxisListType.X, ALU.min)
            nc.scalar.activation(
                weights[b][:], neg_logits[b], ACT.Exp, bias=neg_max[b][:], scale=-1.0, accum_out=row_sum[b][:]
            )
        for b in range(B):
            nc.vector.reciprocal(inv_sum[b][:], row_sum[b][:])
            for piece_b, lo, hi in STORES:
                if piece_b == b:
                    nc.vector.tensor_scalar(
                        result[b][:, lo:hi], weights[b][:, lo:hi], inv_sum[b][:], None, ALU.mult
                    )
                    parts = 2 if (b, hi) == (B - 1, N) else 1
                    for first in range(parts):
                        nc.sync.dma_start(out[b, first:P:parts, lo:hi], result[b][first:P:parts, lo:hi])
